import numpy as np, ml_dtypes
CORES = [23,119,17,113]
N = 4
import mx_ref
BF = ml_dtypes.bfloat16
def entries(a):
    return np.ascontiguousarray(a.T).reshape(-1)
def table(e):
    return np.ascontiguousarray(np.reshape(e, (-1, 16)).T).astype(np.int32)
def cols(t, e):
    v = np.concatenate([t.reshape(128, -1, 4), np.zeros((128, 1, 4), BF)], axis=1)
    return np.ascontiguousarray(v[:, e]).reshape(128, -1)
def f(rng, *shape):
    return mx_ref.flush((rng.standard_normal(shape, dtype=np.float32) * np.exp2(rng.integers(-2, 3, shape[:-1] + (1,)))).astype(BF))
def wide(rng, *shape, cols=0):
    v = rng.standard_normal(shape, dtype=np.float32) * np.exp2(rng.integers(-12, 13, shape)).astype(np.float32)
    if cols: v *= np.repeat(np.exp2(rng.integers(-cols, cols + 1, shape[:-2] + (1, shape[-1] // 4))) * (rng.random(shape[:-2] + (1, shape[-1] // 4)) > 0.0625), 4, axis=-1).astype(np.float32)
    return mx_ref.flush(v.astype(BF))
T, CAPP = 512, 192
def even(n):
    return [T // n + (k < T % n) for k in range(n)]
def counts(rng, h, moves=10 * N * N):
    n = np.array([[h[(d - s) % N] for d in range(N)] for s in range(N)])[rng.permutation(N)][:, rng.permutation(N)]
    top = np.where(n > 0, CAPP, 0)
    for _ in range(moves):
        a, b = rng.permutation(N)[:2]; c, e = rng.permutation(N)[:2]
        k = rng.integers(0, min(n[a, e], n[b, c], top[a, c] - n[a, c], top[b, e] - n[b, e]) + 1)
        n[a, c] += k; n[b, e] += k; n[a, e] -= k; n[b, c] -= k
    return n
def lists(rng, n, back=False):
    a = np.full((N, N, CAPP), -1)
    for s in range(N):
        p = np.arange(T)[::-1] if back else rng.permutation(T)
        for d in range(N):
            k = rng.permutation(CAPP)[:n[s, d]]
            if back: k = np.sort(k)
            a[s, d, k] = p[:n[s, d]]; p = p[n[s, d]:]
    m = []
    for d in range(N):
        k = np.flatnonzero(a[:, d].reshape(-1) >= 0)
        m.append(table(k[::-1] if back else rng.permutation(k)))
    return {"send": np.stack([table(a[s].reshape(-1)) for s in range(N)]), "mine": np.stack(m), "prev": np.stack([m[(r - 1) % N] for r in range(N)])}
def setup_inputs(rng):
    return {"x": f(rng, N, 128, 4 * T), **lists(rng, counts(rng, even(N)))}
def setup_inputs_empty(rng):
    return {**setup_inputs(rng), **lists(rng, counts(rng, even(N - 1) + [0]))}
def setup_inputs_full(rng):
    return {**setup_inputs(rng), **lists(rng, counts(rng, [min(CAPP, max(0, T - k * CAPP)) for k in range(N)], 0))}
def setup_inputs_reversed(rng):
    return {**setup_inputs(rng), **lists(rng, counts(rng, even(N)), back=True)}
def setup_inputs_spread(rng):
    d = setup_inputs(rng); d["x"] = wide(rng, N, 128, 4 * T, cols=8); return d
def check_inputs(d):
    b = []
    v = np.abs(np.asarray(d["x"]).astype(np.float32))
    if not ((v == 0) | ((v >= 2.0 ** -30) & (v <= 2.0 ** 30))).all(): b.append("x")
    for r in range(N):
        c, m = entries(d["send"][r]), entries(d["mine"][r])
        if c.min() < -1 or not np.array_equal(np.sort(c[c >= 0]), np.arange(T)): b.append("send")
        arrived = np.concatenate([entries(d["send"][s])[r * CAPP:(r + 1) * CAPP] for s in range(N)])
        if not np.array_equal(np.sort(m), np.flatnonzero(arrived >= 0)): b.append("mine")
        if not np.array_equal(d["prev"][r], d["mine"][(r - 1) % N]): b.append("prev")
    return b
def reference(x, send, mine, prev):
    K = []
    for r in range(N):
        arrived = np.concatenate([cols(x[s], entries(send[s])[r * CAPP:(r + 1) * CAPP]) for s in range(N)], axis=1)
        K.append(cols(arrived, entries(mine[r])))
    Q = [mx_ref.quantize(t) for t in K]
    y = np.zeros((N, T, 2 * T), np.float32)
    for r in range(N):
        for p in range(T // 128):
            W = mx_ref.quantize(np.ascontiguousarray(K[r][:, 512 * p:512 * p + 512]))
            y[r, 128 * p:128 * p + 128, :T] = mx_ref.matmul(W, Q[r])
            y[r, 128 * p:128 * p + 128, T:] = mx_ref.matmul(W, Q[(r - 1) % N])
    return {"y": y}

@@ -1,0 +1,278 @@
+from concourse.bass import DstId, RemoteDMATransfer, IndirectOffsetOnAxis
+from concourse.mybir import dt, AluOpType, ActivationFunctionType
+
+N, CH, TC = 4, 192, 512
+PAIR = 4 * CH
+CHAIN = 3 * CH
+EMPTY = 100000
+
+SCRATCH = {
+    "xs": ("sbuf", [128, 4 * TC], "bfloat16"),
+    "h": ("sbuf", [128, 4 * N * CH], "bfloat16"),
+    "sl": ("sbuf", [128, 48], "int32"),
+    "so": ("sbuf", [128, 48], "uint16"),
+    "ml": ("sbuf", [128, 64], "int32"),
+    "a1": ("sbuf", [128, 64], "int32"),
+    "a2": ("sbuf", [128, 64], "int32"),
+    "a3": ("sbuf", [128, 64], "int32"),
+    "a4": ("sbuf", [128, 64], "int32"),
+    "a5": ("sbuf", [128, 64], "int32"),
+    "pos": ("sbuf", [128, 64], "int32"),
+    "co": ("sbuf", [128, 64], "uint16"),
+    "b1": ("sbuf", [128, 32], "int32"),
+    "b2": ("sbuf", [128, 32], "int32"),
+    "b3": ("sbuf", [128, 32], "int32"),
+    "b4": ("sbuf", [128, 32], "int32"),
+    "fo": ("sbuf", [128, 32], "uint16"),
+    "num": ("sbuf", [128, TC], "int32"),
+    "inv": ("sbuf", [128, 128 * 9], "int32"),
+    "idx": ("sbuf", [128, 9], "int32"),
+    "c1": ("sbuf", [128, CHAIN + PAIR], "float8_e4m3fn_x4"),
+    "p1": ("sbuf", [128, CHAIN + PAIR], "uint8"),
+    "c2": ("sbuf", [128, PAIR], "float8_e4m3fn_x4"),
+    "p2": ("sbuf", [128, PAIR], "uint8"),
+}
+for _k in range(6):
+    SCRATCH["w%d" % _k] = ("sbuf", [128, 2 * PAIR], "float32")
+    SCRATCH["yb%d" % _k] = ("sbuf", [128, 2 * TC], "float32")
+for _k in range(4):
+    SCRATCH["ps%d" % _k] = ("psum", [128, 1024], "float32")
+
+SEMAPHORES = ["lsem", "xsem", "msem", "isem", "numsem", "v", "s", "t", "near", "far", "sent", "scat"]
+
+
+def rank_program(g, core, T, topo):
+    r = T.rank_of(core)
+    if r is None:
+        return
+    sem = T.sem
+    COPY = ActivationFunctionType.Copy
+    cnt = {"v": 0, "s": 0, "t": 0}
+
+    def tick(q, ins):
+        ins.then_inc(sem[q], 1)
+        cnt[q] += 1
+        return cnt[q]
+
+    V, S, PE = g.vector, g.scalar, g.tensor
+
+    def rising(s):
+        return s < 2
+
+    def place(s, d):
+        half = 0 if rising(s) else 2 * CH
+        if s % 2 == d % 2:
+            return True, (CHAIN if rising(d) else 0) + half
+        return False, half
+
+    win = CHAIN if rising(r) else 0
+    if rising(r):
+        order = [r, r + 1, r + 2, r + 3]
+        src = {1: 0, 2: CH, 3: 2 * CH}
+        qpos = [0, 2 * CH]
+        own = (0, 4 * CH)
+    else:
+        order = [r + 1, r, r + 3, r + 2]
+        src = {1: 5 * CH, 2: 4 * CH, 3: 3 * CH}
+        qpos = [5 * CH, 3 * CH]
+        own = (1, 2 * CH)
+    order = [d % N for d in order]
+
+    for k in range(4):
+        for q, e in ((g.sync, 2 * k), (S, 2 * k + 1)):
+            q.dma_start(T.sl[16 * e:16 * e + 16, :], T.send[:]).then_inc(sem.lsem, 16)
+    g.sync.dma_start(T.xs[0:64, :], T.x[0:64, :]).then_inc(sem.xsem, 16)
+    S.dma_start(T.xs[64:128, :], T.x[64:128, :]).then_inc(sem.xsem, 16)
+    for e in range(8):
+        g.sync.dma_start(T.ml[16 * e:16 * e + 16, 0:32], T.mine[:]).then_inc(sem.msem, 16)
+        g.sync.dma_start(T.ml[16 * e:16 * e + 16, 32:64], T.prev[:]).then_inc(sem.msem, 16)
+
+    g.iota(T.num[:], [[1, TC]], 0, 0).then_inc(sem.numsem, 1)
+
+    v_mem = tick("v", V.memset(T.inv[:], EMPTY))
+    V.wait_ge(sem.lsem, 128)
+    v_off, j = {}, 0
+    while j < N:
+        m = 1
+        while j + m < N and order[j + m] == order[j] + m:
+            m += 1
+        n = tick("v", V.tensor_scalar(T.so[:, 12 * j:12 * (j + m)], T.sl[:, 12 * order[j]:12 * (order[j] + m)],
+                                      0, 4, AluOpType.max, AluOpType.mult))
+        for i in range(m):
+            v_off[j + i] = n
+        j += m
+
+    HW = 4 * 2 * CH
+
+    def gathered(half, t):
+        out = T.h[:, half * HW + t:(half + 1) * HW:4]
+        return out, T.xs[:, t:4 * TC].indirect(T.so[:, 24 * half:24 * half + 24])
+
+    V.wait_ge(sem.v, v_off[1])
+    V.wait_ge(sem.xsem, 32)
+    S.wait_ge(sem.v, v_off[1])
+    S.wait_ge(sem.xsem, 32)
+    vq = []
+    for half in range(2):
+        if half and v_off[3] > v_off[1]:
+            V.wait_ge(sem.v, v_off[3])
+            S.wait_ge(sem.v, v_off[3])
+        for t in (0, 1):
+            vg = tick("v", V.tensor_copy(*gathered(half, t)))
+        for t in (2, 3):
+            sg = tick("s", S.activation(*gathered(half, t), COPY))
+        V.wait_ge(sem.v, vg)
+        V.wait_ge(sem.s, sg)
+        a = qpos[half]
+        vq.append(tick("v", V.quantize_mx(T.c1[:, a:a + 2 * CH], T.p1[:, a:a + 2 * CH],
+                                          T.h[:, half * HW:(half + 1) * HW])))
+    hc, a = own
+    vq.append(tick("v", V.quantize_mx(T.c1[:, a:a + CH], T.p1[:, a:a + CH], T.h[:, 4 * CH * hc:4 * CH * (hc + 1)])))
+
+    dsts = {k: T.cores[(r + k) % N] for k in (1, 2, 3)}
+    feng = topo.engines(core, dsts[1])
+    neng = [e for e in topo.engines(core, dsts[2]) if e not in feng][:4]
+
+    def bits(es):
+        return sum(1 << e for e in es)
+
+    def transfer(k, es, codes):
+        d = (r + k) % N
+        rid, pid, _ = topo.addr(dsts[k])
+        mine_pair, c = place(r, d)
+        a = src[k]
+        if codes:
+            to = T.c1 if mine_pair else T.c2
+            i, o = T.c1[:, a:a + 2 * CH].bitcast(dt.uint8), to[:, c:c + 2 * CH].bitcast(dt.uint8)
+        else:
+            to = T.p1 if mine_pair else T.p2
+            i, o = T.p1[:, a:a + 2 * CH], to[:, c:c + 2 * CH]
+        return RemoteDMATransfer(dst_ids=[DstId(rid=rid, pnc=pid)], dma_engine_mask=bits(es),
+                                 remote_sem=sem.near if mine_pair else sem.far, src=i, dst=o)
+
+    nf, nn = len(feng), len(neng)
+    g.wait_ge(sem.v, vq[0])
+    g.remote_dma_fused([transfer(1, feng, True)], local_sem=sem.sent)
+    g.wait_ge(sem.v, vq[1])
+    g.remote_dma_fused([transfer(3, feng, True), transfer(2, neng, True)], local_sem=sem.sent)
+    g.remote_dma_fused([transfer(1, feng[:nf // 2], False), transfer(3, feng[nf // 2:], False),
+                        transfer(2, neng, False)], local_sem=sem.sent)
+    n_sent = nf + nf + nn + nf + nn
+    n_near, n_far = 2 * nn, 3 * nf
+
+    ge, mul, add = AluOpType.is_ge, AluOpType.mult, AluOpType.add
+    V.wait_ge(sem.msem, 256)
+    tick("v", V.tensor_scalar(T.a1[:], T.ml[:], CH, 3 * CH, ge, mul))
+    tick("v", V.tensor_scalar(T.a2[:, 0:32], T.ml[:, 0:32], 2 * CH, -4 * CH, ge, mul))
+    tick("v", V.tensor_scalar(T.a2[:, 32:64], T.ml[:, 32:64], 2 * CH, -2 * CH, ge, mul))
+    n = tick("v", V.tensor_scalar(T.a3[:], T.ml[:], 3 * CH, 3 * CH, ge, mul))
+    V.wait_ge(sem.v, n)
+    tick("v", V.tensor_tensor(T.a4[:], T.ml[:], T.a2[:], add))
+    n = tick("v", V.tensor_tensor(T.a5[:], T.a1[:], T.a3[:], add))
+    V.wait_ge(sem.v, n)
+    n = tick("v", V.tensor_tensor(T.pos[:], T.a4[:], T.a5[:], add))
+    V.wait_ge(sem.v, n)
+    tick("v", V.tensor_scalar(T.b1[:], T.pos[:, 0:32], 127, None, AluOpType.bitwise_and))
+    n = tick("v", V.tensor_scalar(T.b2[:], T.pos[:, 0:32], 7, None, AluOpType.arith_shift_right))
+    v_co = tick("v", V.tensor_copy(T.co[:], T.pos[:]))
+    V.wait_ge(sem.v, n)
+    n = tick("v", V.tensor_scalar(T.b3[:], T.b1[:], 9, None, mul))
+    V.wait_ge(sem.v, n)
+    n = tick("v", V.tensor_tensor(T.b4[:], T.b3[:], T.b2[:], add))
+    V.wait_ge(sem.v, n)
+    n = tick("v", V.tensor_copy(T.fo[:], T.b4[:]))
+    V.wait_ge(sem.numsem, 1)
+    V.wait_ge(sem.v, n)
+    v_inv = tick("v", V.tensor_copy(T.inv[:, 0:1152].indirect(T.fo[:, 0:32]), T.num[:]))
+    g.sync.wait_ge(sem.v, v_inv)
+    g.sync.dma_start(T.idx[:], T.inv[0:1, :]).then_inc(sem.isem, 16)
+
+    PS = [T["ps%d" % u] for u in range(4)]
+    me = r % 2
+    blocks = [3 * me + i for i in range(3)] + [3 * (1 - me) + i for i in range(3)]
+    W = [T["w%d" % b] for b in blocks]
+    Y = [T["yb%d" % b] for b in blocks]
+    icol = [6 * (b // 3) + b % 3 for b in blocks]
+    NC, FC = PAIR * me, PAIR * (1 - me)
+
+    def near(a, b):
+        return T.c1[:, win + a:win + b], T.p1[:, win + a:win + b]
+
+    def far(a, b):
+        return T.c2[:, a:b], T.p2[:, a:b]
+
+    def product(j, side, u, cuts):
+        st = (near if j < 3 else far)(CH + 128 * (j % 3), CH + 128 * (j % 3) + 128)
+        done = []
+        for k, (a, b) in enumerate(cuts):
+            mv = side(a, b)
+            done.append(tick("t", PE.matmul_mx(PS[u][:, 512 * k:512 * k + b - a], st[0], st[1], mv[0], mv[1],
+                                               True, True)))
+        return done
+
+    BIG, EVEN = [(0, 512), (512, PAIR)], [(0, 2 * CH), (2 * CH, PAIR)]
+
+    PE.wait_ge(sem.v, vq[2])
+    PE.wait_ge(sem.near, n_near)
+    t_near = [product(j, near, j, BIG)[-1] for j in range(3)]
+    s_near = []
+    for j in range(3):
+        S.wait_ge(sem.t, t_near[j])
+        s_near.append(tick("s", S.activation(W[j][:, NC:NC + PAIR], PS[j][:, 0:PAIR], COPY)))
+    PE.wait_ge(sem.far, n_far)
+
+    v_cp, s_cp, v_ga, s_ga = {}, {}, {}, {}
+
+    def empty(vn, sn):
+        if vn:
+            PE.wait_ge(sem.v, vn)
+        if sn:
+            PE.wait_ge(sem.s, sn)
+
+    def leave_split(j, u):
+        ta, tb = product(j, far, u, EVEN)
+        V.wait_ge(sem.t, ta)
+        v_cp[j] = tick("v", V.tensor_copy(W[j][:, FC:FC + 2 * CH], PS[u][:, 0:2 * CH]))
+        S.wait_ge(sem.t, tb)
+        s_cp[j] = tick("s", S.activation(W[j][:, FC + 2 * CH:FC + PAIR], PS[u][:, 512:512 + 2 * CH], COPY))
+
+    def leave_whole(j, un, uf, before_n, before_f):
+        empty(*before_n)
+        tn = product(j, near, un, BIG)[-1]
+        S.wait_ge(sem.t, tn)
+        s_cp[j] = tick("s", S.activation(W[j][:, NC:NC + PAIR], PS[un][:, 0:PAIR], COPY))
+        empty(*before_f)
+        tf = product(j, far, uf, BIG)[-1]
+        V.wait_ge(sem.t, tf)
+        v_cp[j] = tick("v", V.tensor_copy(W[j][:, FC:FC + PAIR], PS[uf][:, 0:PAIR]))
+
+    def columns(j):
+        for q in (V, S):
+            q.wait_ge(sem.v, max(v_cp[j], v_co))
+            q.wait_ge(sem.s, s_cp[j])
+        s_ga[j] = tick("s", S.activation(Y[j][:, 0:TC], W[j][:, CH:2 * PAIR].indirect(T.co[:, 0:32]), COPY))
+        v_ga[j] = tick("v", V.tensor_copy(Y[j][:, TC:2 * TC], W[j][:, 0:2 * PAIR].indirect(T.co[:, 32:64])))
+
+    leave_split(0, 3)
+    columns(0)
+    empty(0, s_near[0])
+    leave_split(1, 0)
+    empty(0, s_near[1])
+    leave_split(2, 1)
+    columns(1)
+    leave_whole(3, 2, 3, (0, s_near[2]), (v_cp[0], s_cp[0]))
+    columns(2)
+    leave_whole(4, 0, 1, (v_cp[1], s_cp[1]), (v_cp[2], s_cp[2]))
+    columns(3)
+    leave_whole(5, 2, 3, (0, s_cp[3]), (v_cp[3], 0))
+    columns(4)
+    columns(5)
+
+    g.wait_ge(sem.isem, 16)
+    for j in range(6):
+        g.wait_ge(sem.v, v_ga[j])
+        g.wait_ge(sem.s, s_ga[j])
+        g.indirect_dma_start(T.y[:], IndirectOffsetOnAxis(ap=T.idx[:, icol[j]:icol[j] + 1], axis=0), Y[j][:], None,
+                             bounds_check=TC - 1, oob_is_err=False).then_inc(sem.scat, 16)
+    g.wait_ge(sem.sent, n_sent)
+    g.wait_ge(sem.scat, 96)

@@ -2,8 +2,10 @@ from concourse.bass import DstId, RemoteDMATransfer, IndirectOffsetOnAxis
 from concourse.mybir import dt, AluOpType, ActivationFunctionType
 
 N, CH, TC = 4, 192, 512
-PAIR = 4 * CH
+RUN = 2 * CH
+PAIR = 2 * RUN
 CHAIN = 3 * CH
+FIRST = 128
 EMPTY = 100000
 
 SCRATCH = {
@@ -12,17 +14,8 @@ SCRATCH = {
     "sl": ("sbuf", [128, 48], "int32"),
     "so": ("sbuf", [128, 48], "uint16"),
     "ml": ("sbuf", [128, 64], "int32"),
-    "a1": ("sbuf", [128, 64], "int32"),
-    "a2": ("sbuf", [128, 64], "int32"),
-    "a3": ("sbuf", [128, 64], "int32"),
-    "a4": ("sbuf", [128, 64], "int32"),
-    "a5": ("sbuf", [128, 64], "int32"),
     "pos": ("sbuf", [128, 64], "int32"),
     "co": ("sbuf", [128, 64], "uint16"),
-    "b1": ("sbuf", [128, 32], "int32"),
-    "b2": ("sbuf", [128, 32], "int32"),
-    "b3": ("sbuf", [128, 32], "int32"),
-    "b4": ("sbuf", [128, 32], "int32"),
     "fo": ("sbuf", [128, 32], "uint16"),
     "num": ("sbuf", [128, TC], "int32"),
     "inv": ("sbuf", [128, 128 * 9], "int32"),
@@ -32,13 +25,17 @@ SCRATCH = {
     "c2": ("sbuf", [128, PAIR], "float8_e4m3fn_x4"),
     "p2": ("sbuf", [128, PAIR], "uint8"),
 }
+for _k in range(1, 6):
+    SCRATCH["a%d" % _k] = ("sbuf", [128, 64], "int32")
+for _k in range(1, 5):
+    SCRATCH["b%d" % _k] = ("sbuf", [128, 32], "int32")
 for _k in range(6):
     SCRATCH["w%d" % _k] = ("sbuf", [128, 2 * PAIR], "float32")
     SCRATCH["yb%d" % _k] = ("sbuf", [128, 2 * TC], "float32")
 for _k in range(4):
     SCRATCH["ps%d" % _k] = ("psum", [128, 1024], "float32")
 
-SEMAPHORES = ["lsem", "xsem", "msem", "isem", "numsem", "v", "s", "t", "near", "far", "sent", "scat"]
+SEMAPHORES = ["lsem", "xsem", "msem", "gsem", "isem", "numsem", "v", "s", "t", "near", "far1", "far3", "sent", "scat"]
 
 
 def rank_program(g, core, T, topo):
@@ -60,7 +57,7 @@ def rank_program(g, core, T, topo):
         return s < 2
 
     def place(s, d):
-        half = 0 if rising(s) else 2 * CH
+        half = 0 if rising(s) else RUN
         if s % 2 == d % 2:
             return True, (CHAIN if rising(d) else 0) + half
         return False, half
@@ -71,11 +68,13 @@ def rank_program(g, core, T, topo):
         src = {1: 0, 2: CH, 3: 2 * CH}
         qpos = [0, 2 * CH]
         own = (0, 4 * CH)
+        parts = [(0, FIRST), (FIRST, RUN)]
     else:
         order = [r + 1, r, r + 3, r + 2]
         src = {1: 5 * CH, 2: 4 * CH, 3: 3 * CH}
         qpos = [5 * CH, 3 * CH]
         own = (1, 2 * CH)
+        parts = [(RUN - FIRST, RUN), (0, RUN - FIRST)]
     order = [d % N for d in order]
 
     for k in range(4):
@@ -85,11 +84,13 @@ def rank_program(g, core, T, topo):
     S.dma_start(T.xs[64:128, :], T.x[64:128, :]).then_inc(sem.xsem, 16)
     for e in range(8):
         g.sync.dma_start(T.ml[16 * e:16 * e + 16, 0:32], T.mine[:]).then_inc(sem.msem, 16)
+    for e in range(7):
         g.sync.dma_start(T.ml[16 * e:16 * e + 16, 32:64], T.prev[:]).then_inc(sem.msem, 16)
+    g.dma_start(T.ml[112:128, 32:64], T.prev[:]).then_inc(sem.gsem, 16)
 
     g.iota(T.num[:], [[1, TC]], 0, 0).then_inc(sem.numsem, 1)
 
-    v_mem = tick("v", V.memset(T.inv[:], EMPTY))
+    tick("v", V.memset(T.inv[:], EMPTY))
     V.wait_ge(sem.lsem, 128)
     v_off, j = {}, 0
     while j < N:
@@ -102,66 +103,68 @@ def rank_program(g, core, T, topo):
             v_off[j + i] = n
         j += m
 
-    HW = 4 * 2 * CH
+    def gathered(t, a, b):
+        return T.h[:, 4 * a + t:4 * b:4], T.xs[:, t:4 * TC].indirect(T.so[:, a // 16:b // 16])
 
-    def gathered(half, t):
-        out = T.h[:, half * HW + t:(half + 1) * HW:4]
-        return out, T.xs[:, t:4 * TC].indirect(T.so[:, 24 * half:24 * half + 24])
-
-    V.wait_ge(sem.v, v_off[1])
     V.wait_ge(sem.xsem, 32)
-    S.wait_ge(sem.v, v_off[1])
     S.wait_ge(sem.xsem, 32)
-    vq = []
-    for half in range(2):
-        if half and v_off[3] > v_off[1]:
-            V.wait_ge(sem.v, v_off[3])
-            S.wait_ge(sem.v, v_off[3])
-        for t in (0, 1):
-            vg = tick("v", V.tensor_copy(*gathered(half, t)))
-        for t in (2, 3):
-            sg = tick("s", S.activation(*gathered(half, t), COPY))
+    vq, seen = [], 0
+    for c0, c1 in parts + [(RUN, 2 * RUN)]:
+        n = max(v_off[i // CH] for i in range(c0, c1, 64))
+        if n > seen:
+            V.wait_ge(sem.v, n)
+            S.wait_ge(sem.v, n)
+            seen = n
+        if c0 < RUN:
+            vjobs, sjobs = [(0, c0, c1), (1, c0, c1)], [(2, c0, c1), (3, c0, c1)]
+        else:
+            vjobs = [(0, c0, c1), (1, c0, c0 + CH)]
+            sjobs = [(2, c0, c1), (3, c0, c1), (1, c0 + CH, c1)]
+        for job in vjobs:
+            vg = tick("v", V.tensor_copy(*gathered(*job)))
+        for job in sjobs:
+            sg = tick("s", S.activation(*gathered(*job), COPY))
         V.wait_ge(sem.v, vg)
         V.wait_ge(sem.s, sg)
-        a = qpos[half]
-        vq.append(tick("v", V.quantize_mx(T.c1[:, a:a + 2 * CH], T.p1[:, a:a + 2 * CH],
-                                          T.h[:, half * HW:(half + 1) * HW])))
+        a = qpos[0] + c0 if c0 < RUN else qpos[1]
+        vq.append(tick("v", V.quantize_mx(T.c1[:, a:a + c1 - c0], T.p1[:, a:a + c1 - c0], T.h[:, 4 * c0:4 * c1])))
     hc, a = own
     vq.append(tick("v", V.quantize_mx(T.c1[:, a:a + CH], T.p1[:, a:a + CH], T.h[:, 4 * CH * hc:4 * CH * (hc + 1)])))
 
     dsts = {k: T.cores[(r + k) % N] for k in (1, 2, 3)}
     feng = topo.engines(core, dsts[1])
-    neng = [e for e in topo.engines(core, dsts[2]) if e not in feng][:4]
+    neng = [e for e in topo.engines(core, dsts[2]) if e not in feng]
+    lands = {1: sem.far1, 2: sem.near, 3: sem.far3}
 
-    def bits(es):
-        return sum(1 << e for e in es)
-
-    def transfer(k, es, codes):
-        d = (r + k) % N
+    def transfer(k, es, codes, m=0, n=RUN):
         rid, pid, _ = topo.addr(dsts[k])
-        mine_pair, c = place(r, d)
-        a = src[k]
+        same_pair, c = place(r, (r + k) % N)
+        a, c = src[k] + m, c + m
         if codes:
-            to = T.c1 if mine_pair else T.c2
-            i, o = T.c1[:, a:a + 2 * CH].bitcast(dt.uint8), to[:, c:c + 2 * CH].bitcast(dt.uint8)
+            to = T.c1 if same_pair else T.c2
+            i, o = T.c1[:, a:a + n].bitcast(dt.uint8), to[:, c:c + n].bitcast(dt.uint8)
         else:
-            to = T.p1 if mine_pair else T.p2
-            i, o = T.p1[:, a:a + 2 * CH], to[:, c:c + 2 * CH]
-        return RemoteDMATransfer(dst_ids=[DstId(rid=rid, pnc=pid)], dma_engine_mask=bits(es),
-                                 remote_sem=sem.near if mine_pair else sem.far, src=i, dst=o)
+            to = T.p1 if same_pair else T.p2
+            i, o = T.p1[:, a:a + n], to[:, c:c + n]
+        return RemoteDMATransfer(dst_ids=[DstId(rid=rid, pnc=pid)], dma_engine_mask=sum(1 << e for e in es),
+                                 remote_sem=lands[k], src=i, dst=o)
 
-    nf, nn = len(feng), len(neng)
-    g.wait_ge(sem.v, vq[0])
-    g.remote_dma_fused([transfer(1, feng, True)], local_sem=sem.sent)
-    g.wait_ge(sem.v, vq[1])
-    g.remote_dma_fused([transfer(3, feng, True), transfer(2, neng, True)], local_sem=sem.sent)
-    g.remote_dma_fused([transfer(1, feng[:nf // 2], False), transfer(3, feng[nf // 2:], False),
-                        transfer(2, neng, False)], local_sem=sem.sent)
-    n_sent = nf + nf + nn + nf + nn
-    n_near, n_far = 2 * nn, 3 * nf
+    few = feng[:len(feng) // 2]
+    nf, nn, n1 = len(feng), len(neng), len(few)
+    for i, es in enumerate((few, feng)):
+        c0, c1 = parts[i]
+        g.wait_ge(sem.v, vq[i])
+        g.remote_dma_fused([transfer(1, es, True, c0, c1 - c0)], local_sem=sem.sent)
+    g.remote_dma_fused([transfer(1, feng, False)], local_sem=sem.sent)
+    g.wait_ge(sem.v, vq[2])
+    for codes in (True, False):
+        g.remote_dma_fused([transfer(3, feng, codes), transfer(2, neng, codes)], local_sem=sem.sent)
+    n_far1, n_far3, n_near = n1 + 2 * nf, 2 * nf, 2 * nn
+    n_sent = n_far1 + n_far3 + n_near
 
     ge, mul, add = AluOpType.is_ge, AluOpType.mult, AluOpType.add
-    V.wait_ge(sem.msem, 256)
+    V.wait_ge(sem.msem, 240)
+    V.wait_ge(sem.gsem, 16)
     tick("v", V.tensor_scalar(T.a1[:], T.ml[:], CH, 3 * CH, ge, mul))
     tick("v", V.tensor_scalar(T.a2[:, 0:32], T.ml[:, 0:32], 2 * CH, -4 * CH, ge, mul))
     tick("v", V.tensor_scalar(T.a2[:, 32:64], T.ml[:, 32:64], 2 * CH, -2 * CH, ge, mul))
@@ -194,6 +197,8 @@ def rank_program(g, core, T, topo):
     Y = [T["yb%d" % b] for b in blocks]
     icol = [6 * (b // 3) + b % 3 for b in blocks]
     NC, FC = PAIR * me, PAIR * (1 - me)
+    A0 = 0 if rising((r - 1) % N) else RUN
+    B0 = RUN - A0
 
     def near(a, b):
         return T.c1[:, win + a:win + b], T.p1[:, win + a:win + b]
@@ -201,72 +206,55 @@ def rank_program(g, core, T, topo):
     def far(a, b):
         return T.c2[:, a:b], T.p2[:, a:b]
 
-    def product(j, side, u, cuts):
+    def product(j, side, u, bank, a, b):
         st = (near if j < 3 else far)(CH + 128 * (j % 3), CH + 128 * (j % 3) + 128)
-        done = []
-        for k, (a, b) in enumerate(cuts):
-            mv = side(a, b)
-            done.append(tick("t", PE.matmul_mx(PS[u][:, 512 * k:512 * k + b - a], st[0], st[1], mv[0], mv[1],
-                                               True, True)))
-        return done
+        mv = side(a, b)
+        return tick("t", PE.matmul_mx(PS[u][:, 512 * bank:512 * bank + b - a], st[0], st[1], mv[0], mv[1], True, True))
 
-    BIG, EVEN = [(0, 512), (512, PAIR)], [(0, 2 * CH), (2 * CH, PAIR)]
+    v_ga, s_ga = {}, {}
+    readers = {}
 
-    PE.wait_ge(sem.v, vq[2])
-    PE.wait_ge(sem.near, n_near)
-    t_near = [product(j, near, j, BIG)[-1] for j in range(3)]
-    s_near = []
-    for j in range(3):
-        S.wait_ge(sem.t, t_near[j])
-        s_near.append(tick("s", S.activation(W[j][:, NC:NC + PAIR], PS[j][:, 0:PAIR], COPY)))
-    PE.wait_ge(sem.far, n_far)
+    def free(u):
+        for q, n in readers.get(u, ()):
+            PE.wait_ge(sem[q], n)
 
-    v_cp, s_cp, v_ga, s_ga = {}, {}, {}, {}
+    def half(j, side, u):
+        free(u)
+        product(j, side, u, 0, 0, 512)
+        return product(j, side, u, 1, 512, PAIR)
 
-    def empty(vn, sn):
-        if vn:
-            PE.wait_ge(sem.v, vn)
-        if sn:
-            PE.wait_ge(sem.s, sn)
+    def by_scalar(j, u, bank, w, n, t):
+        S.wait_ge(sem.t, t)
+        return tick("s", S.activation(W[j][:, w:w + n], PS[u][:, 512 * bank:512 * bank + n], COPY))
 
-    def leave_split(j, u):
-        ta, tb = product(j, far, u, EVEN)
-        V.wait_ge(sem.t, ta)
-        v_cp[j] = tick("v", V.tensor_copy(W[j][:, FC:FC + 2 * CH], PS[u][:, 0:2 * CH]))
-        S.wait_ge(sem.t, tb)
-        s_cp[j] = tick("s", S.activation(W[j][:, FC + 2 * CH:FC + PAIR], PS[u][:, 512:512 + 2 * CH], COPY))
+    def by_vector(j, u, bank, w, n, t):
+        V.wait_ge(sem.t, t)
+        return tick("v", V.tensor_copy(W[j][:, w:w + n], PS[u][:, 512 * bank:512 * bank + n]))
 
-    def leave_whole(j, un, uf, before_n, before_f):
-        empty(*before_n)
-        tn = product(j, near, un, BIG)[-1]
-        S.wait_ge(sem.t, tn)
-        s_cp[j] = tick("s", S.activation(W[j][:, NC:NC + PAIR], PS[un][:, 0:PAIR], COPY))
-        empty(*before_f)
-        tf = product(j, far, uf, BIG)[-1]
-        V.wait_ge(sem.t, tf)
-        v_cp[j] = tick("v", V.tensor_copy(W[j][:, FC:FC + PAIR], PS[uf][:, 0:PAIR]))
-
-    def columns(j):
+    def columns(j, vn, sn):
         for q in (V, S):
-            q.wait_ge(sem.v, max(v_cp[j], v_co))
-            q.wait_ge(sem.s, s_cp[j])
+            q.wait_ge(sem.v, max(vn, v_co))
+            q.wait_ge(sem.s, sn)
         s_ga[j] = tick("s", S.activation(Y[j][:, 0:TC], W[j][:, CH:2 * PAIR].indirect(T.co[:, 0:32]), COPY))
         v_ga[j] = tick("v", V.tensor_copy(Y[j][:, TC:2 * TC], W[j][:, 0:2 * PAIR].indirect(T.co[:, 32:64])))
 
-    leave_split(0, 3)
-    columns(0)
-    empty(0, s_near[0])
-    leave_split(1, 0)
-    empty(0, s_near[1])
-    leave_split(2, 1)
-    columns(1)
-    leave_whole(3, 2, 3, (0, s_near[2]), (v_cp[0], s_cp[0]))
-    columns(2)
-    leave_whole(4, 0, 1, (v_cp[1], s_cp[1]), (v_cp[2], s_cp[2]))
-    columns(3)
-    leave_whole(5, 2, 3, (0, s_cp[3]), (v_cp[3], 0))
-    columns(4)
-    columns(5)
+    PE.wait_ge(sem.v, vq[3])
+    PE.wait_ge(sem.near, n_near)
+    readers[0] = (("s", by_scalar(0, 0, 0, NC, PAIR, half(0, near, 0))),)
+    PE.wait_ge(sem.far1, n_far1)
+    readers[2] = (("v", by_vector(0, 2, 0, FC + A0, RUN, product(0, far, 2, 0, A0, A0 + RUN))),)
+    PE.wait_ge(sem.far3, n_far3)
+    vn = by_vector(0, 3, 0, FC + B0, CH, product(0, far, 3, 0, B0, B0 + CH))
+    sn = by_scalar(0, 3, 1, FC + B0 + CH, CH, product(0, far, 3, 1, B0 + CH, B0 + RUN))
+    readers[3] = (("v", vn), ("s", sn))
+    columns(0, vn, sn)
+    for j in range(1, 6):
+        u = 2 * (1 - j % 2)
+        sn = by_scalar(j, u, 0, NC, PAIR, half(j, near, u))
+        readers[u] = (("s", sn),)
+        vn = by_vector(j, u + 1, 0, FC, PAIR, half(j, far, u + 1))
+        readers[u + 1] = (("v", vn),)
+        columns(j, vn, sn)
 
     g.wait_ge(sem.isem, 16)
     for j in range(6):

from concourse.bass import DstId, RemoteDMATransfer, IndirectOffsetOnAxis
from concourse.mybir import dt, AluOpType, ActivationFunctionType

N, CH, TC = 4, 192, 512
RUN = 2 * CH
PAIR = 2 * RUN
CHAIN = 3 * CH
FIRST = 128
EMPTY = 100000

SCRATCH = {
    "xs": ("sbuf", [128, 4 * TC], "bfloat16"),
    "h": ("sbuf", [128, 4 * N * CH], "bfloat16"),
    "sl": ("sbuf", [128, 48], "int32"),
    "so": ("sbuf", [128, 48], "uint16"),
    "ml": ("sbuf", [128, 64], "int32"),
    "pos": ("sbuf", [128, 64], "int32"),
    "co": ("sbuf", [128, 64], "uint16"),
    "fo": ("sbuf", [128, 32], "uint16"),
    "num": ("sbuf", [128, TC], "int32"),
    "inv": ("sbuf", [128, 128 * 9], "int32"),
    "idx": ("sbuf", [128, 9], "int32"),
    "c1": ("sbuf", [128, CHAIN + PAIR], "float8_e4m3fn_x4"),
    "p1": ("sbuf", [128, CHAIN + PAIR], "uint8"),
    "c2": ("sbuf", [128, PAIR], "float8_e4m3fn_x4"),
    "p2": ("sbuf", [128, PAIR], "uint8"),
}
for _k in range(1, 6):
    SCRATCH["a%d" % _k] = ("sbuf", [128, 64], "int32")
for _k in range(1, 5):
    SCRATCH["b%d" % _k] = ("sbuf", [128, 32], "int32")
for _k in range(6):
    SCRATCH["w%d" % _k] = ("sbuf", [128, 2 * PAIR], "float32")
    SCRATCH["yb%d" % _k] = ("sbuf", [128, 2 * TC], "float32")
for _k in range(4):
    SCRATCH["ps%d" % _k] = ("psum", [128, 1024], "float32")

SEMAPHORES = ["lsem", "xsem", "msem", "gsem", "isem", "numsem", "v", "s", "t", "near", "far1", "far3", "sent", "scat"]


def rank_program(g, core, T, topo):
    r = T.rank_of(core)
    if r is None:
        return
    sem = T.sem
    COPY = ActivationFunctionType.Copy
    cnt = {"v": 0, "s": 0, "t": 0}

    def tick(q, ins):
        ins.then_inc(sem[q], 1)
        cnt[q] += 1
        return cnt[q]

    V, S, PE = g.vector, g.scalar, g.tensor

    def rising(s):
        return s < 2

    def place(s, d):
        half = 0 if rising(s) else RUN
        if s % 2 == d % 2:
            return True, (CHAIN if rising(d) else 0) + half
        return False, half

    win = CHAIN if rising(r) else 0
    if rising(r):
        order = [r, r + 1, r + 2, r + 3]
        src = {1: 0, 2: CH, 3: 2 * CH}
        qpos = [0, 2 * CH]
        own = (0, 4 * CH)
        parts = [(0, FIRST), (FIRST, RUN)]
    else:
        order = [r + 1, r, r + 3, r + 2]
        src = {1: 5 * CH, 2: 4 * CH, 3: 3 * CH}
        qpos = [5 * CH, 3 * CH]
        own = (1, 2 * CH)
        parts = [(RUN - FIRST, RUN), (0, RUN - FIRST)]
    order = [d % N for d in order]

    for k in range(4):
        for q, e in ((g.sync, 2 * k), (S, 2 * k + 1)):
            q.dma_start(T.sl[16 * e:16 * e + 16, :], T.send[:]).then_inc(sem.lsem, 16)
    g.sync.dma_start(T.xs[0:64, :], T.x[0:64, :]).then_inc(sem.xsem, 16)
    S.dma_start(T.xs[64:128, :], T.x[64:128, :]).then_inc(sem.xsem, 16)
    for e in range(8):
        g.sync.dma_start(T.ml[16 * e:16 * e + 16, 0:32], T.mine[:]).then_inc(sem.msem, 16)
    for e in range(7):
        g.sync.dma_start(T.ml[16 * e:16 * e + 16, 32:64], T.prev[:]).then_inc(sem.msem, 16)
    g.dma_start(T.ml[112:128, 32:64], T.prev[:]).then_inc(sem.gsem, 16)

    g.iota(T.num[:], [[1, TC]], 0, 0).then_inc(sem.numsem, 1)

    tick("v", V.memset(T.inv[:], EMPTY))
    V.wait_ge(sem.lsem, 128)
    v_off, j = {}, 0
    while j < N:
        m = 1
        while j + m < N and order[j + m] == order[j] + m:
            m += 1
        n = tick("v", V.tensor_scalar(T.so[:, 12 * j:12 * (j + m)], T.sl[:, 12 * order[j]:12 * (order[j] + m)],
                                      0, 4, AluOpType.max, AluOpType.mult))
        for i in range(m):
            v_off[j + i] = n
        j += m

    def gathered(t, a, b):
        return T.h[:, 4 * a + t:4 * b:4], T.xs[:, t:4 * TC].indirect(T.so[:, a // 16:b // 16])

    V.wait_ge(sem.xsem, 32)
    S.wait_ge(sem.xsem, 32)
    vq, seen = [], 0
    for c0, c1 in parts + [(RUN, 2 * RUN)]:
        n = max(v_off[i // CH] for i in range(c0, c1, 64))
        if n > seen:
            V.wait_ge(sem.v, n)
            S.wait_ge(sem.v, n)
            seen = n
        if c0 < RUN:
            vjobs, sjobs = [(0, c0, c1), (1, c0, c1)], [(2, c0, c1), (3, c0, c1)]
        else:
            vjobs = [(0, c0, c1), (1, c0, c0 + CH)]
            sjobs = [(2, c0, c1), (3, c0, c1), (1, c0 + CH, c1)]
        for job in vjobs:
            vg = tick("v", V.tensor_copy(*gathered(*job)))
        for job in sjobs:
            sg = tick("s", S.activation(*gathered(*job), COPY))
        V.wait_ge(sem.v, vg)
        V.wait_ge(sem.s, sg)
        a = qpos[0] + c0 if c0 < RUN else qpos[1]
        vq.append(tick("v", V.quantize_mx(T.c1[:, a:a + c1 - c0], T.p1[:, a:a + c1 - c0], T.h[:, 4 * c0:4 * c1])))
    hc, a = own
    vq.append(tick("v", V.quantize_mx(T.c1[:, a:a + CH], T.p1[:, a:a + CH], T.h[:, 4 * CH * hc:4 * CH * (hc + 1)])))

    dsts = {k: T.cores[(r + k) % N] for k in (1, 2, 3)}
    feng = topo.engines(core, dsts[1])
    neng = [e for e in topo.engines(core, dsts[2]) if e not in feng]
    lands = {1: sem.far1, 2: sem.near, 3: sem.far3}

    def transfer(k, es, codes, m=0, n=RUN):
        rid, pid, _ = topo.addr(dsts[k])
        same_pair, c = place(r, (r + k) % N)
        a, c = src[k] + m, c + m
        if codes:
            to = T.c1 if same_pair else T.c2
            i, o = T.c1[:, a:a + n].bitcast(dt.uint8), to[:, c:c + n].bitcast(dt.uint8)
        else:
            to = T.p1 if same_pair else T.p2
            i, o = T.p1[:, a:a + n], to[:, c:c + n]
        return RemoteDMATransfer(dst_ids=[DstId(rid=rid, pnc=pid)], dma_engine_mask=sum(1 << e for e in es),
                                 remote_sem=lands[k], src=i, dst=o)

    few = feng[:len(feng) // 2]
    nf, nn, n1 = len(feng), len(neng), len(few)
    for i, es in enumerate((few, feng)):
        c0, c1 = parts[i]
        g.wait_ge(sem.v, vq[i])
        g.remote_dma_fused([transfer(1, es, True, c0, c1 - c0)], local_sem=sem.sent)
    g.remote_dma_fused([transfer(1, feng, False)], local_sem=sem.sent)
    g.wait_ge(sem.v, vq[2])
    for codes in (True, False):
        g.remote_dma_fused([transfer(3, feng, codes), transfer(2, neng, codes)], local_sem=sem.sent)
    n_far1, n_far3, n_near = n1 + 2 * nf, 2 * nf, 2 * nn
    n_sent = n_far1 + n_far3 + n_near

    ge, mul, add = AluOpType.is_ge, AluOpType.mult, AluOpType.add
    V.wait_ge(sem.msem, 240)
    V.wait_ge(sem.gsem, 16)
    tick("v", V.tensor_scalar(T.a1[:], T.ml[:], CH, 3 * CH, ge, mul))
    tick("v", V.tensor_scalar(T.a2[:, 0:32], T.ml[:, 0:32], 2 * CH, -4 * CH, ge, mul))
    tick("v", V.tensor_scalar(T.a2[:, 32:64], T.ml[:, 32:64], 2 * CH, -2 * CH, ge, mul))
    n = tick("v", V.tensor_scalar(T.a3[:], T.ml[:], 3 * CH, 3 * CH, ge, mul))
    V.wait_ge(sem.v, n)
    tick("v", V.tensor_tensor(T.a4[:], T.ml[:], T.a2[:], add))
    n = tick("v", V.tensor_tensor(T.a5[:], T.a1[:], T.a3[:], add))
    V.wait_ge(sem.v, n)
    n = tick("v", V.tensor_tensor(T.pos[:], T.a4[:], T.a5[:], add))
    V.wait_ge(sem.v, n)
    tick("v", V.tensor_scalar(T.b1[:], T.pos[:, 0:32], 127, None, AluOpType.bitwise_and))
    n = tick("v", V.tensor_scalar(T.b2[:], T.pos[:, 0:32], 7, None, AluOpType.arith_shift_right))
    v_co = tick("v", V.tensor_copy(T.co[:], T.pos[:]))
    V.wait_ge(sem.v, n)
    n = tick("v", V.tensor_scalar(T.b3[:], T.b1[:], 9, None, mul))
    V.wait_ge(sem.v, n)
    n = tick("v", V.tensor_tensor(T.b4[:], T.b3[:], T.b2[:], add))
    V.wait_ge(sem.v, n)
    n = tick("v", V.tensor_copy(T.fo[:], T.b4[:]))
    V.wait_ge(sem.numsem, 1)
    V.wait_ge(sem.v, n)
    v_inv = tick("v", V.tensor_copy(T.inv[:, 0:1152].indirect(T.fo[:, 0:32]), T.num[:]))
    g.sync.wait_ge(sem.v, v_inv)
    g.sync.dma_start(T.idx[:], T.inv[0:1, :]).then_inc(sem.isem, 16)

    PS = [T["ps%d" % u] for u in range(4)]
    me = r % 2
    blocks = [3 * me + i for i in range(3)] + [3 * (1 - me) + i for i in range(3)]
    W = [T["w%d" % b] for b in blocks]
    Y = [T["yb%d" % b] for b in blocks]
    icol = [6 * (b // 3) + b % 3 for b in blocks]
    NC, FC = PAIR * me, PAIR * (1 - me)
    A0 = 0 if rising((r - 1) % N) else RUN
    B0 = RUN - A0

    def near(a, b):
        return T.c1[:, win + a:win + b], T.p1[:, win + a:win + b]

    def far(a, b):
        return T.c2[:, a:b], T.p2[:, a:b]

    def product(j, side, u, bank, a, b):
        st = (near if j < 3 else far)(CH + 128 * (j % 3), CH + 128 * (j % 3) + 128)
        mv = side(a, b)
        return tick("t", PE.matmul_mx(PS[u][:, 512 * bank:512 * bank + b - a], st[0], st[1], mv[0], mv[1], True, True))

    v_ga, s_ga = {}, {}
    readers = {}

    def free(u):
        for q, n in readers.get(u, ()):
            PE.wait_ge(sem[q], n)

    def half(j, side, u):
        free(u)
        product(j, side, u, 0, 0, 512)
        return product(j, side, u, 1, 512, PAIR)

    def by_scalar(j, u, bank, w, n, t):
        S.wait_ge(sem.t, t)
        return tick("s", S.activation(W[j][:, w:w + n], PS[u][:, 512 * bank:512 * bank + n], COPY))

    def by_vector(j, u, bank, w, n, t):
        V.wait_ge(sem.t, t)
        return tick("v", V.tensor_copy(W[j][:, w:w + n], PS[u][:, 512 * bank:512 * bank + n]))

    def columns(j, vn, sn):
        for q in (V, S):
            q.wait_ge(sem.v, max(vn, v_co))
            q.wait_ge(sem.s, sn)
        s_ga[j] = tick("s", S.activation(Y[j][:, 0:TC], W[j][:, CH:2 * PAIR].indirect(T.co[:, 0:32]), COPY))
        v_ga[j] = tick("v", V.tensor_copy(Y[j][:, TC:2 * TC], W[j][:, 0:2 * PAIR].indirect(T.co[:, 32:64])))

    PE.wait_ge(sem.v, vq[3])
    PE.wait_ge(sem.near, n_near)
    readers[0] = (("s", by_scalar(0, 0, 0, NC, PAIR, half(0, near, 0))),)
    PE.wait_ge(sem.far1, n_far1)
    readers[2] = (("v", by_vector(0, 2, 0, FC + A0, RUN, product(0, far, 2, 0, A0, A0 + RUN))),)
    PE.wait_ge(sem.far3, n_far3)
    vn = by_vector(0, 3, 0, FC + B0, CH, product(0, far, 3, 0, B0, B0 + CH))
    sn = by_scalar(0, 3, 1, FC + B0 + CH, CH, product(0, far, 3, 1, B0 + CH, B0 + RUN))
    readers[3] = (("v", vn), ("s", sn))
    columns(0, vn, sn)
    for j in range(1, 6):
        u = 2 * (1 - j % 2)
        sn = by_scalar(j, u, 0, NC, PAIR, half(j, near, u))
        readers[u] = (("s", sn),)
        vn = by_vector(j, u + 1, 0, FC, PAIR, half(j, far, u + 1))
        readers[u + 1] = (("v", vn),)
        columns(j, vn, sn)

    g.wait_ge(sem.isem, 16)
    for j in range(6):
        g.wait_ge(sem.v, v_ga[j])
        g.wait_ge(sem.s, s_ga[j])
        g.indirect_dma_start(T.y[:], IndirectOffsetOnAxis(ap=T.idx[:, icol[j]:icol[j] + 1], axis=0), Y[j][:], None,
                             bounds_check=TC - 1, oob_is_err=False).then_inc(sem.scat, 16)
    g.wait_ge(sem.sent, n_sent)
    g.wait_ge(sem.scat, 96)
